import numpy as np, ml_dtypes
CORES = [2,3,42,43,82,83,122,123]
N = 8
BF = ml_dtypes.bfloat16
def gentries(a):
    return np.ascontiguousarray(a.reshape(8, 16, -1).transpose(0, 2, 1)).reshape(8, -1)
def gtable(e):
    e = np.asarray(e); return np.ascontiguousarray(e.reshape(8, -1, 16).transpose(0, 2, 1)).reshape(128, -1).astype(np.int32)
A, B, RO, DB, XM = 1024, 128, 2, 4, (1, 4)
P = 3 * A + B
def tie(L, u, v):
    L[u] = v; L[v] = u
def net(rng, nf, pairs, nb, how=""):
    o = rng.permutation(A); k = 3 * A + rng.permutation(B); L = np.arange(P); e = nf + 2 * pairs
    if how == "ends":
        o = o[(o != 0) & (o != A - 1)]; k = k[(k != 3 * A) & (k != P - 1)]
        o = np.concatenate([o[:e], [0, A - 1], o[e:]]); k = np.concatenate([[3 * A, P - 1], k])
    fr, a, b, bd, w = o[:nf], o[nf:nf + pairs], o[nf + pairs:e], o[e:e + nb], o[e + nb:]
    tie(L, a, b); tie(L, bd, k[:nb])
    if how == "chains":
        j = 0; M = 2 ** DB
        for m, shut in ((M - 1, 0), (M, 0), (M + 1, 0), (2 * M, 0), (1, 0), (1, 1), (3, 1), (M + 1, 0)):
            for i in (1, 2):
                tie(L, i * A + b[j:j + m - 1], i * A + a[j + 1:j + m])
                if shut: tie(L, i * A + b[j + m - 1], i * A + a[j])
            j += m
    if how == "selves": tie(L, A + bd, 2 * A + bd)
    if how == "mates": tie(L, A + bd[:nb // 2], A + bd[nb // 2:nb // 2 * 2])
    h = 0 if how in ("selves", "mates") else min(nb, len(w)) * 3 // 4
    tie(L, w[:h], A + bd[:h])
    idle = L == np.arange(P)
    for i in range(3): idle[i * A + fr] = False
    aux = rng.permutation(A + np.flatnonzero(idle[A:3 * A])); n = len(w) - h
    tie(L, w[h:], aux[:n])
    rest = rng.permutation(np.concatenate([aux[n:], 3 * A + np.flatnonzero(idle[3 * A:])])); n = len(rest) // 2
    tie(L, rest[:n], rest[n:2 * n])
    return L, a, b
def sizes(rng):
    nf = int(rng.integers(A // 8, A // 4 + 1)); nb = int(rng.integers(5 * B // 8, 7 * B // 8 + 1)); nw = int(rng.integers(A // 16, A // 8 + 1))
    return nf, (A - nf - nb - nw) // 2, nb
def blank(rng):
    return np.zeros((N, 8, P), np.int64), rng.integers(0, 16, (N, 8, 16, A)), rng.integers(2, 9, (N, 8, 16, RO))
def manned(v):
    at = v[3 * A:]
    return (at < A) & (v[np.minimum(at, A - 1)] == 3 * A + np.arange(B))
def pack(L, x, t):
    return {"lk": np.stack([gtable(v) for v in L]), "x0": np.ascontiguousarray(x.reshape(N, 128, A)).astype(np.int32), "th": np.ascontiguousarray(t.reshape(N, 128, RO)).astype(np.int32)}
def setup_inputs(rng):
    L, x, t = blank(rng)
    for r in range(N):
        for g in range(8): L[r, g] = net(rng, *sizes(rng))[0]
    return pack(L, x, t)
def setup_inputs_chains(rng):
    L, x, t = blank(rng); M = 2 ** DB
    for r in range(N):
        for g in range(8):
            c = (g + r) % 4; nf, n, nb = sizes(rng)
            if c % 2 == 1:
                L[r, g] = net(rng, nf, n, nb)[0]; continue
            if c == 2:
                n = n + nf // 2; nf = 0; t[r, g, :, 0] = 0; t[r, g, :, 1] = 15
            else: t[r, g, :, 0] = 15
            v, a, b = net(rng, nf, n, nb, "chains")
            to = np.array([i * A + p for i in (1, 2) for p in (a[M - 1], a[3 * M], a[5 * M + 1], a[5 * M + 2], b[5 * M + 3], a[5 * M + 5])])
            k = 3 * A + rng.permutation(np.flatnonzero(v[3 * A:] >= A))[:len(to)]
            v[k] = to; L[r, g] = v
            xa = rng.integers(0, 2, (16, M)); xa[0] = 1
            x[r, g][:, a[M - 1:2 * M - 1]] = xa; x[r, g][:, b[M - 1:2 * M - 1]] = rng.integers(14, 16, (16, M))
            x[r, g][:, a[6 * M + 5]] = 0; x[r, g][:, b[6 * M + 5]] = 15
    return pack(L, x, t)
def setup_inputs_room(rng):
    L, x, t = blank(rng); f = A // 8
    for r in range(0, N, 2):
        for g in range(8):
            n = A // 4
            nf, c = ((f, f // 2), (f, f // 2 + 1), (f, f // 2 - 1), (f, 0), (0, f // 2), (1, f // 2), (f + 1, f // 2), (f + 1, f // 2 + 1))[(g + r) % 8]
            L[r, g], a, b = net(rng, nf, n, 3 * B // 4); t[r, g, :, 0] = 5
            xa = rng.integers(0, 16, (16, n)); xb = xa ^ 1; m = rng.permutation(n)[:c]
            xa[:, m] = xa[:, m] & 7; xb[:, m] = xa[:, m] + 8
            x[r, g][:, a] = xa; x[r, g][:, b] = xb
    for r in range(1, N, 2):
        t[r] = rng.integers(1, 8, (8, 16, RO))
        for g in range(8):
            if g == (r + 3) % 8:
                L[r, g] = net(rng, A // 2, A // 4, 0)[0]; t[r, g, :, 0] = 0; t[r, g, :, 1:] = 15; continue
            if g == (r + 4) % 8:
                L[r, g] = net(rng, 0, A // 2, 0)[0]; t[r, g, :, 0] = 15; t[r, g, :, 1:] = 0; continue
            L[r, g], a, b = net(rng, *sizes(rng)); n = len(a); j = np.arange(n)
            xa = rng.integers(0, 8, (16, n)); xb = xa + t[r, g, :, :1]; i = rng.integers(0, 16, n)
            xb[i, j] = xb[i, j] + rng.integers(-1, 2, n)
            if g == (r + 1) % 8:
                t[r, g] = 0; xb = np.where(rng.random(n) < 0.5, xa, xb)
            if g == (r + 2) % 8:
                t[r, g] = 15; xa = np.zeros((16, n), np.int64); xb = xa + 15; xb[i, j] = 14 + rng.integers(0, 2, n)
            x[r, g][:, a] = xa; x[r, g][:, b] = xb
    return pack(L, x, t)
def setup_inputs_border(rng):
    L, x, t = blank(rng); s = int(rng.integers(0, 8))
    for r in range(N):
        for g in range(8):
            how = ("full", "none", "odd", "selves", "mates", "few", "ends", "")[(g + s) % 8]; nf, n, nb = sizes(rng)
            if how == "full" or (how == "odd" and r % 2 == 1): nb = B
            elif how == "none" or how == "odd": nb = 0
            elif how == "few": nb = B // 8
            L[r, g] = net(rng, nf, (A - nf - nb - A // 16) // 2, nb, how)[0]
    return pack(L, x, t)
def setup_inputs_loose(rng):
    L, x, t = blank(rng); z = int(rng.integers(0, 8))
    for g in range(8):
        kk = 3 * A + rng.permutation(B)
        for r in range(N):
            if g == (z + r) % 8:
                L[r, g] = rng.integers(0, P, P); continue
            nf = sizes(rng)[0]; nb = 7 * B // 8
            v, a, b = net(rng, nf, (A - nf - nb - A // 4) // 2, nb)
            fr = np.flatnonzero(v[:A] == np.arange(A)); w = rng.permutation(np.flatnonzero((v[:A] >= A) & (v[:A] < 3 * A)))
            s = B // 8 + r * (B // 16)
            k = np.concatenate([kk[:B // 8], kk[s:s + B // 8]])
            hold = np.ones(P, bool); hold[k] = False
            m = 3 * A + np.flatnonzero((v[3 * A:] < A) & hold[3 * A:]); bd = v[m]
            kind = np.arange(len(k)) % 4
            v[k] = np.where(kind == 0, rng.choice(w, len(k)), np.where(kind == 1, rng.choice(np.concatenate([a, b]), len(k)), np.where(kind == 2, rng.choice(bd, len(k)), rng.choice(fr, len(k)))))
            n = len(w) // 2; kind = np.arange(n) % 3
            v[w[:n]] = np.where(kind == 0, rng.choice(np.concatenate([a, b]), n), np.where(kind == 1, rng.choice(bd, n), rng.choice(m, n)))
            q = A + rng.permutation(2 * A)[:A // 4]
            v[q] = rng.integers(0, 3, len(q)) * A + rng.choice(np.concatenate([fr, a, b]), len(q))
            L[r, g] = v
    for r in range(N):
        q = r ^ XM[0]
        for g in range(8):
            if r > q or g in ((z + r) % 8, (z + q) % 8): continue
            v = L[r, g]; k = int(rng.choice(np.flatnonzero(manned(v) & manned(L[q, g]))))
            v[A - 1] = 3 * A + k; v[3 * A + k] = 2 * A - 1
            k = 3 * A + rng.permutation(np.flatnonzero(manned(v) & manned(L[q, g])))[:8]; c = np.array(v[k])
            v[A + c[:4]] = c[np.array([1, 2, 0, 3])]
            h = np.array(v[:A]); a = np.flatnonzero((h < A) & (h > np.arange(A)) & (v[np.minimum(h, A - 1)] == np.arange(A)))
            a = rng.permutation(a)[:4]; b = np.array(v[a])
            v[k[4:]] = A + a; v[A + b] = c[4:]; x[r, g][:, b] = x[r, g][:, a] ^ 1
    return pack(L, x, t)
def setup_inputs_spread(rng):
    L, x, t = blank(rng)
    x = np.minimum((np.exp2(4.2 * rng.random((N, 8, 1, A))) * rng.random((N, 8, 16, A))).astype(np.int64), 15)
    t = np.minimum((np.exp2(4 * rng.random((N, 8, 16, RO))) * rng.random((N, 8, 16, RO))).astype(np.int64), 15)
    for r in range(N):
        for g in range(8):
            nf = int(rng.integers(0, A // 2)); nb = int(rng.integers(0, B + 1)); nw = int(rng.integers(0, A // 4))
            L[r, g] = net(rng, nf, (A - nf - nb - nw) // 2, nb)[0]
    return pack(L, x, t)
def check_inputs(d):
    bad = []
    for k, hi in (("lk", P - 1), ("x0", 15), ("th", 15)):
        if np.min(d[k]) < 0 or np.max(d[k]) > hi: bad.append("range of " + k)
    return bad
def meet(L, ph, x, th):
    own = np.arange(P); col = np.arange(A); q = L[:A]; c = np.minimum(q, A - 1)
    pair = (q < A) & (q != col) & (L[c] == col)
    dif = np.abs(x - x[:, c]); near = np.add.reduce(dif, axis=0) < th
    free = np.flatnonzero(q == col)
    a = np.flatnonzero(pair & near); b = q[a]
    u = np.flatnonzero(pair & ~near & (col < q))[:len(free) // 2]; v = q[u]
    f1 = free[0:2 * len(u):2]; f2 = free[1:2 * len(u):2]
    J = np.arange(P); S = np.zeros((16, P), np.int64)
    for i in (1, 2):
        J[i * A + a] = L[i * A + b]; S[:, i * A + a] = (ph[:, i * A + b] + dif[:, a]) & 15
    J[A + u] = v; J[2 * A + u] = f1; J[A + v] = u; J[2 * A + v] = f2
    for k in range(DB):
        S = (S + S[:, J]) & 15; J = J[J]
    to = J[L]; ps = (ph + S[:, L]) & 15
    nl = np.array(to); nph = np.array(ps); nx = np.array(x)
    for new, old in ((u, A + v), (v, A + u), (f1, 2 * A + u), (f2, 2 * A + v)):
        nl[new] = to[old]; nph[:, new] = ps[:, old]
    for e, f in ((A + u, A + v), (2 * A + u, A + f1), (2 * A + v, A + f2), (2 * A + f1, 2 * A + f2)):
        nl[e] = f; nl[f] = e; nph[:, e] = 0; nph[:, f] = 0
    for i in range(3):
        nl[i * A + a] = own[i * A + a]; nph[:, i * A + a] = 0
    nx[:, f1] = (x[:, u] + x[:, v]) & 15; nx[:, f2] = dif[:, u]
    return nl, nph, nx
def border(L, ph, x, m):
    at = L[:, :, 3 * A:]; up = (at < A) & (np.take_along_axis(L, np.minimum(at, A - 1), 2) == 3 * A + np.arange(B))
    nl = np.array(L); nph = np.array(ph); nx = np.array(x)
    for r in range(N):
        q = r ^ m
        for g in range(8):
            k = np.flatnonzero(up[r, g] & up[q, g]); a = at[r, g][k]; b = at[q, g][k]
            rho = np.arange(P); rho[a] = A + a; rho[A + a] = a
            nl[r, g] = rho[L[r, g][rho]]
            n = ph[r, g][:, rho]; s = (ph[r, g][:, 3 * A + k] + ph[q, g][:, 3 * A + k]) & 15
            n[:, 3 * A + k] = s; n[:, A + a] = s; nph[r, g] = n
            nx[r, g][:, a] = x[q, g][:, b]
    return nl, nph, nx
def reference(lk, x0, th):
    L = np.stack([gentries(v) for v in lk]).astype(np.int64); x = x0.astype(np.int64).reshape(N, 8, 16, A); ph = np.zeros((N, 8, 16, P), np.int64)
    t = np.add.reduce(th.astype(np.int64).reshape(N, 8, 16, RO), axis=2)
    for rnd in range(RO):
        for r in range(N):
            for g in range(8):
                L[r, g], ph[r, g], x[r, g] = meet(L[r, g], ph[r, g], x[r, g], t[r, g, rnd])
        L, ph, x = border(L, ph, x, XM[rnd])
    return {"yl": L.astype(np.float32), "yp": ph.reshape(N, 128, P).astype(np.float32).astype(BF), "yx": x.reshape(N, 128, A).astype(np.float32).astype(BF)}

import numpy as np
from concourse.bass import DstId, RemoteDMATransfer
from concourse.mybir import dt, AluOpType, AxisListType, ActivationFunctionType

A, NB, P = 1024, 128, 3200
XM = (1, 4)
DUM, LW, I1, I2, T2, I1B, IPB, G1, TAB, IDP, JA, IDB, BIGN = (
    0, 256, 3456, 4480, 5504, 6016, 7040, 8064, 9088, 12176, 13200, 15248, 15376)
X0, XS, XZ, XD, XL, XN = 256, 1296, 1808, 1824, 2848, 3872
H0, HZ, HD, HB, HN = 272, 3344, 3360, 3488, 3616
NW, NU, NI, NH = 7900, 3800, 704, 1300

SCRATCH = {
    "big": ("sbuf", [128, BIGN], "bfloat16"), "jb": ("sbuf", [128, P], "bfloat16"),
    "rho0": ("sbuf", [128, 3456], "bfloat16"), "rho1": ("sbuf", [128, 3456], "float32"),
    "ylb": ("sbuf", [128, 3456], "float32"),
    "idc": ("sbuf", [128, A], "bfloat16"), "lpn": ("sbuf", [128, A], "bfloat16"),
    "lp": ("sbuf", [128, A + 16], "bfloat16"), "lr": ("sbuf", [128, 2176], "bfloat16"),
    "mp": ("sbuf", [128, A], "bfloat16"),
    "xw0": ("sbuf", [128, XN], "bfloat16"), "xw1": ("sbuf", [128, XN], "bfloat16"),
    "xw2": ("sbuf", [128, XS], "bfloat16"),
    "xi": ("sbuf", [128, A], "int32"), "lki": ("sbuf", [128, 200], "int32"), "thi": ("sbuf", [128, 4], "int32"),
    "dtm": ("sbuf", [128, A], "bfloat16"), "difm": ("sbuf", [128, A], "bfloat16"),
    "sa": ("sbuf", [128, 16 + P], "float32"), "sb": ("sbuf", [128, 16 + P], "float32"),
    "sc0": ("sbuf", [128, 2 * A], "float32"), "sc1": ("sbuf", [128, 2 * A], "float32"),
    "ph1": ("sbuf", [128, HN], "bfloat16"), "hsrc": ("sbuf", [128, A], "bfloat16"),
    "qi": ("sbuf", [128, P], "int32"), "ypb": ("sbuf", [128, HN], "bfloat16"),
    "w": ("sbuf", [128, NW], "float32"), "u": ("sbuf", [128, NU], "uint16"),
    "n": ("sbuf", [128, NI], "int32"), "h": ("sbuf", [128, NH], "bfloat16"),
    "dlo": ("sbuf", [128, 200], "bfloat16"), "dhi": ("sbuf", [128, 200], "bfloat16"),
    "bf": ("sbuf", [128, 128], "float32"),
    "cd0": ("sbuf", [128, 256], "bfloat16"), "cd1": ("sbuf", [128, 256], "float32"),
    "sw0": ("sbuf", [128, 256], "bfloat16"), "sw1": ("sbuf", [128, 256], "float32"),
}
for _k in ("eall", "e01", "e23"):
    SCRATCH[_k] = ("sbuf", [128, 144], "bfloat16")
for _k in ("b2", "bm", "b01", "tl", "tlf", "tlc", "rcp0", "rcp1"):
    SCRATCH[_k] = ("sbuf", [128, 128], "bfloat16")
for _k in ("sp0", "sp1"):
    SCRATCH[_k] = ("sbuf", [128, 256], "bfloat16")
for _k in ("snd0", "snd1", "rcv0", "rcv1"):
    SCRATCH[_k] = ("sbuf", [128, 152], "bfloat16")
for _k in range(8):
    SCRATCH["ps%d" % _k] = ("psum", [128, 512], "float32")
SEMAPHORES = ["eV", "eS", "eP", "eG"] + ["d%d" % k for k in range(80)] + ["r%d" % k for k in range(4)]

AL = AluOpType
AF = ActivationFunctionType
NOM = dict(cy=1.04, c=1.56, s=3.8, pe=0.7, ov=60.0, oa=80.0, lat=110.0, dma=2000.0, bw=160.0, rem=3000.0)
CFG = dict(cl=1024, cv=1024, cc=512, seed=2, heat=500.0, its=38000)


def size(r):
    return len(range(r[1], r[2], r[3] if len(r) > 3 else 1))


def two(r):
    return SCRATCH[r[0]][2] in ("bfloat16", "uint16")


def inps(r):
    return SCRATCH[r[0]][0] == "psum"


def ap(T, r):
    if len(r) > 3:
        return T[r[0]][:, r[1]:r[2]:r[3]]
    return T[r[0]][:, r[1]:r[2]]


def val(T, s):
    return ap(T, s) if isinstance(s, tuple) else s


def sub(r, a, b):
    return (r[0], r[1] + a, r[1] + b)


def slot(r, k, n):
    return (r[0], r[1] + k, r[2], n, k)


def build(cfg):
    ops = []
    top = {"w": 0, "u": 0, "n": 0, "h": 0}
    named = {}

    def tile(name, n=64, pool="w"):
        if name not in named:
            named[name] = (pool, top[pool], top[pool] + n)
            top[pool] += (n + 7) // 8 * 8
        return named[name]

    def op(name, eng, cost, rd, wr, emit):
        ops.append(dict(name=name, eng=eng, cost=cost, rd=[r for r in rd if isinstance(r, tuple)], wr=wr, emit=emit))

    def ew(out, ins, f):
        n = size(out)
        if f == 2 and any(inps(r) for r in ins):
            f = 1
        elif f == 1 and two(out) and all(two(r) for r in ins):
            f = 0.5
        return ("ew", max(64, n * f), max(64, n))

    def ts(out, a, s1, o0, s2=None, o1=None):
        def e(g, T, q):
            if o1 is None:
                return g.vector.tensor_scalar(ap(T, out), ap(T, a), val(T, s1), None, o0)
            return g.vector.tensor_scalar(ap(T, out), ap(T, a), val(T, s1), val(T, s2), o0, o1)
        op("ts", "V", ew(out, [a], 1), [a, s1, s2], [out], e)
        return out

    def aff(out, a, m, c, eng="SV"):
        def e(g, T, q):
            if q == "V":
                return g.vector.tensor_scalar(ap(T, out), ap(T, a), val(T, m), val(T, c), AL.mult, AL.add)
            return g.scalar.activation(ap(T, out), ap(T, a), AF.Identity, bias=val(T, c), scale=val(T, m))
        op("aff", eng, ew(out, [a], 1), [a, m, c], [out], e)
        return out

    def add(out, a, c):
        return aff(out, a, 1.0, c if isinstance(c, tuple) else float(c))

    def tt(out, a, b, o):
        op("tt", "V", ew(out, [a, b], 2), [a, b], [out],
           lambda g, T, q: g.vector.tensor_tensor(ap(T, out), ap(T, a), ap(T, b), o))
        return out

    def cp(out, a):
        op("cp", "V", ew(out, [a], 1), [a], [out], lambda g, T, q: g.vector.tensor_copy(ap(T, out), ap(T, a)))
        return out

    def scan(out, d0, d1, o0, o1):
        op("scan", "V", ew(out, [d0, d1], 1), [d0, d1], [out],
           lambda g, T, q: g.vector.tensor_tensor_scan(ap(T, out), ap(T, d0), ap(T, d1), 0.0, o0, o1))
        return out

    def pick(name, pat, vals, n):
        return slot(scan(tile(name, 64 * n), pat, vals, AL.mult, AL.max), n - 1, n)

    def mset(out, c):
        op("mset", "V", ew(out, [], 1), [], [out], lambda g, T, q: g.vector.memset(ap(T, out), c))
        return out

    def iota(out, pat, base, cm):
        def e(g, T, q):
            if SCRATCH[out[0]][2] == "int32":
                return g.iota(ap(T, out), pat, base, cm)
            return g.iota(ap(T, out), pat, base, cm, allow_small_or_imprecise_dtypes=True)
        op("iota", "G", ("g", 130.0, 2 * size(out)), [], [out], e)
        return out

    def zero(out):
        iota(out, [[0, size(out)]], 0, 0)
        if size(out) > 200:
            ops[-1]["rd"] = [("tlc", 0, 128), ("tlf", 0, 128), named["c212"], named["aw0"]]
        return out

    def asel(out, a, cmp, fill):
        op("asel", "G", ("g", 170.0, 256), [a], [out],
           lambda g, T, q: g.affine_select(ap(T, out), ap(T, a), [[-1, 128]], cmp, fill, 0, 1))

    def chunks(n, ch):
        return [(a, min(a + ch, n)) for a in range(0, n, ch)]

    def gat(out, win, lst, plus=None, o=AL.add, eng="SV", ch=None, name="gat"):
        for a, b in chunks(size(out), ch or (cfg["cl"] if plus is None else cfg["cv"])):
            def e(g, T, q, a=a, b=b):
                src = ap(T, win).indirect(ap(T, sub(lst, a // 16, b // 16)))
                if plus is not None:
                    return g.vector.tensor_tensor(ap(T, sub(out, a, b)), src, ap(T, sub(plus, a, b)), o)
                if q == "V":
                    return g.vector.tensor_copy(ap(T, sub(out, a, b)), src)
                return g.scalar.activation(ap(T, sub(out, a, b)), src, AF.Copy)
            rd = [win, sub(lst, a // 16, b // 16)] + ([sub(plus, a, b)] if plus is not None else [])
            op(name, "V" if plus is not None else eng, ("gat", b - a), rd, [sub(out, a, b)], e)

    def scat(win, lst, a, b=None):
        def e(g, T, q):
            dst = ap(T, win).indirect(ap(T, lst))
            if b is None:
                return g.vector.tensor_copy(dst, ap(T, a))
            return g.vector.tensor_tensor(dst, ap(T, a), ap(T, b), AL.add)
        op("scat", "V", ("scat", size(a)), [lst, a, b], [win], e)

    def mm(out, terms):
        def e(g, T, q):
            for k, (l, r) in enumerate(terms):
                last = g.tensor.matmul(ap(T, out), ap(T, l), ap(T, r), k == 0, k == len(terms) - 1)
            return last
        cyc = sum(max(64, size(r)) * (1 if two(r) else 4) for l, r in terms)
        op("mm", "P", ("pe", cyc), [t for lr in terms for t in lr], [out], e)
        return out

    def wrap(out, src, E="e01", step=1):
        return mm(out, [((E, 15 - i, 143 - i), (src[0], src[1] + step * i, src[2], 16 * step)) for i in range(16)])

    def dma(q, fo, fi, rd, wr, nbytes):
        op("dma", q, ("dma", nbytes), rd, wr,
           lambda g, T, qq: (g.sync if qq == "Y" else g.scalar).dma_start(fo(T), fi(T)))

    def move(dst, src):
        dma("Y", lambda T: ap(T, dst), lambda T: ap(T, src), [src], [dst], size(src) * (256 if two(src) else 512))

    def twin(dst, src):
        for s, e in chunks(size(src), cfg["cc"]):
            def em(g, T, q, d=sub(dst, s, e), r=sub(src, s, e)):
                if q == "Y":
                    return g.sync.dma_start(ap(T, d), ap(T, r))
                if q == "V":
                    return g.vector.tensor_copy(ap(T, d), ap(T, r))
                return g.scalar.activation(ap(T, d), ap(T, r), AF.Copy)
            op("twin", "YSV", ("twin", e - s, 0.5 if two(src) else 1.0), [sub(src, s, e)], [sub(dst, s, e)], em)
        return dst

    def remote(k, rnd, src, dst):
        op("send", "G", ("send", k, rnd), [src], [], (src, dst))
        op("recv", "R", ("recv", k, len(ops) - 1), [], [dst], None)

    def ps(k, a, b):
        return ("ps%d" % k, a, b)

    def u16(name, a, c=None, o=AL.add):
        out = tile(name, size(a), "u")
        return cp(out, a) if c is None else ts(out, a, float(c), o)

    dma("Y", lambda T: T.lki[:, :], lambda T: T.lk[:, :], [], [("lki", 0, 200)], 102400)
    dma("S", lambda T: T.xi[:, :], lambda T: T.x0[:, :], [], [("xi", 0, A)], 524288)
    dma("Y", lambda T: T.thi[:, 0:2], lambda T: T.th[:, :], [], [("thi", 0, 4)], 1024)
    mset(("big", LW, I1), 0.0)
    ki = iota(tile("ki", 1, "n"), [[0, 1]], 0, 1)
    ic = cp(tile("ic", 1), ts(tile("ii", 1, "n"), ki, 15, AL.bitwise_and))
    m01 = ts(tile("m01", 1), ic, 2.0, AL.is_lt)
    m03 = ts(tile("m03", 1), ic, 4.0, AL.is_lt)
    m23 = tt(tile("m23", 1), m03, m01, AL.subtract)
    hi = tt(tile("hi", 1), ts(tile("kio", 1, "n"), ki, 1, AL.bitwise_and), m03, AL.mult)
    lo = tt(tile("lo", 1), m03, hi, AL.subtract)
    hcs = ts(tile("hcs", 49), iota(tile("hc0", 49), [[64, 49]], 0, 0), hi, AL.mult)
    hc = {c: sub(hcs, c // 64, c // 64 + 1) for c in range(0, 3073, 64)}
    v8 = iota(tile("v8", 128), [[-16, 8], [0, 16]], 0, 1)
    bf = tt(("bf", 0, 128), ts(ps(4, 0, 128), v8, 0.0, AL.is_ge), ts(tile("l16", 128), v8, 15.0, AL.is_le), AL.mult)
    for E, m in (("eall", 1.0), ("e01", m01), ("e23", m23)):
        zero((E, 0, 144))
        aff((E, 15, 143, 16), ("bf", 0, 128, 16), m, 0.0)
    b2 = aff(("b2", 0, 128), bf, 2.0, 0.0)
    aff(("bm", 0, 128), bf, -2.0, 0.0)
    aff(("b01", 0, 128), bf, m01, 0.0)
    asel(("tl", 0, 128), ("bm", 0, 128), AL.is_gt, 0.0)
    asel(("tlf", 0, 128), ("tl", 0, 128), AL.not_equal, 4096.0)
    asel(("tlc", 0, 128), ("tl", 0, 128), AL.not_equal, 3072.0)
    aw = add(tile("aw", 200), iota(tile("aw0", 200), [[16, 200]], 0, 0), ic)
    a = sub(aw, 0, 64)
    kw = sub(aw, 192, 200)
    m64 = iota(tile("m64"), [[1, 64]], 0, 0)
    ones = iota(tile("ones", 64, "h"), [[0, 64]], 1, 0)
    c212 = iota(tile("c212", 64, "h"), [[0, 64]], 212, 0)
    aff(("big", IDP, IDP + 64), m64, lo, 0.0)
    for c in (64, 128, 256, 512):
        add(("big", IDP + c, IDP + 2 * c), ("big", IDP, IDP + c), hc[c])
    idp = ("big", IDP, JA)
    add(("big", I1, I2), idp, hc[1024])
    add(("big", I2, T2), idp, hc[2048])
    add(("big", IDB, BIGN), sub(idp, 0, 128), hc[3072])
    aff(("idc", 0, A), idp, m23, 0.0)
    move(("big", IPB, G1), idp)
    move(("big", I1B, IPB), ("big", I1, I2))
    move(("jb", 0, A), idp)
    move(("jb", 3 * A, P), ("big", IDB, BIGN))
    PJ, PK, PM, PU = tile("PJ", 192), tile("PK", 256), tile("PM", 256), tile("PU", 128)
    for r, n in ((PJ, 3), (PK, 4), (PM, 4), (PU, 2)):
        aff(slot(r, 0, n), a, 0.0, 0.0)
    for r in (("big", TAB, IDP), ("big", T2, I1B), ("big", DUM, LW), ("xw0", XZ, XD), ("xw1", XZ, XD), ("sa", 0, 8),
              ("sa", 16, 16 + A), ("sa", 16 + 3 * A, 16 + P), ("sb", 16, 16 + A), ("sb", 16 + 3 * A, 16 + P),
              ("lp", A, A + 16), ("xw1", 0, X0), ("xw1", X0 + A, XS), ("xw0", X0 + A, XS), ("rho0", 0, 3456),
              ("ph1", 0, H0), ("ph1", HZ, HB), ("xw2", 0, X0), ("xw2", X0 + A, XS), ("ypb", 0, H0),
              ("ypb", HZ, HB), ("ylb", 0, 256)):
        zero(r)
    iota(("sa", 8, 16), [[0, 8]], -65536, 0)
    for i in (0, 1):
        for (s, e, d) in ((IDP, JA, 256), (I1, T2, 256 + A), (IDB, BIGN, 256 + 3 * A)):
            dma("Y", lambda T, i=i, s=s, e=e, d=d: T.rho0[i:128:16, d:d + e - s],
                lambda T, i=i, s=s, e=e: T.big[i:128:16, s:e], [("big", s, e)], [("rho0", d, d + e - s, 1, i)], 16 * (e - s))
    aff(("sw0", 128, 256), ("big", IDB, BIGN), m01, 0.0)
    iota(("sw1", 128, 256), [[1, 128]], 3 * A, 0)
    iota(("rho1", 0, 3456), [[1, 3456]], -256, 0)
    a1, a78 = add(tile("a1"), a, 1), add(tile("a78"), a, 7809)
    pv = [ps(3, 64 * k, 64 * k + 64) for k in range(8)]
    av, a16 = cp(pv[0], a), aff(pv[1], a, 1.0, 16.0, eng="V")
    VJ1, VJ2, VK1, VK2, VM, VX = (tile("VJ1", 192), tile("VJ2", 192), tile("VK1", 256), tile("VK2", 256),
                                  tile("VM", 256), tile("VX", 128))
    add(slot(VJ1, 1, 3), a, I1 - LW)
    add(slot(VJ2, 1, 3), a, I2 - LW)
    add(slot(VK1, 3, 4), a, 0)
    add(slot(VK2, 3, 4), a, A)
    add(slot(VM, 3, 4), a, 0)
    add(slot(VX, 1, 2), a, 0)
    V24, K24 = tile("V24", 24), tile("K24", 24)
    for r, c in ((sub(V24, 16, 24), 128), (sub(K24, 0, 8), 0), (sub(K24, 8, 16), 128), (sub(K24, 16, 24), 0)):
        add(r, kw, c - 3 * A)
    h01 = tt(tile("h01", 1), hc[1024], m01, AL.mult)
    thr = cp(tile("thr", 2), mm(ps(2, 300, 302), [(bf, cp(tile("thf", 2), ("thi", 0, 2)))]))

    lki = ("lki", 0, 200)
    Lw = cp(tile("Lw", 200), lki)
    dlo = cp(("dlo", 0, 200), ts(tile("nlo", 200, "n"), lki, 63, AL.bitwise_and))
    dhi = tt(("dhi", 0, 200), Lw, dlo, AL.subtract)
    dma("Y", lambda T: T.big[0:128:16, LW:I1], lambda T: T.dlo[:, :], [dlo], [("big", LW, I1, 1, 0)], 51200)
    dma("S", lambda T: T.big[1:128:16, LW:I1], lambda T: T.dhi[:, :], [dhi], [("big", LW, I1, 1, 1)], 51200)
    cp(("xw0", X0, X0 + A), ("xi", 0, A))
    pa16 = u16("pa16", add(tile("pa"), m64, aff(tile("i200", 1), ic, 200.0, 0.0)))

    def turn(name, src):
        ints = cp(tile("pi", 64, "n"), src)
        l4 = ts(tile("pl", 64, "n"), ints, 15, AL.bitwise_and)
        h4 = ts(tile("ph", 64, "n"), ints, 4, AL.arith_shift_right)
        return tt(tile(name), ts(pv[4], l4, 200.0, AL.mult), h4, AL.add)

    for rd in (0, 1):
        R = str(rd)
        xw, xn = "xw%d" % rd, "xw%d" % (rd + 1)
        x = (xw, X0, X0 + A)
        SEC = 64 if rd == 0 else A
        q = sub(Lw, 0, 64)
        ql = u16("ql" + R, q, 1023, AL.min)
        qc = ts(tile("qc"), q, 1023.0, AL.min)
        if rd == 0:
            locq = turn("locq", qc)
            gat((xw, XL, XN), ("big", LW, I1), u16("lq0", locq), name="LQ")
            Lp = ("lpn", 0, A)
            gat(Lp, ("big", LW, I1), pa16, name="Lpn")
            xsrc, xtwo = ("xi", 0, A), x
        else:
            locq, Lp, xsrc, xtwo = qc, ("big", LW, LW + A), x, twin(("difm", 0, A), x)
            gat((xw, XL, XN), Lp, ql, name="LQ")
        gat(("dtm", 0, A), xsrc, ql, xtwo, AL.subtract, ch=512, name="xq")
        for s, e in chunks(A, 512):
            op("abs", "S", ("ew", e - s, e - s), [("dtm", s, e)], [(xw, XD + s, XD + e)],
               lambda g, T, qq, s=s, e=e, xw=xw: g.scalar.activation(T[xw][:, XD + s:XD + e], T.dtm[:, s:e], AF.Abs))
        LQ = wrap(ps(7, 0, 64), (xw, XL, XN))
        D = wrap(ps(0, 0, 64), (xw, XD, XL), "eall")
        free = tt(tile("free", 64, "h"), q, av, AL.is_equal)
        csf = scan(tile("csf", 64, "h"), ones, free, AL.mult, AL.add)
        RF = mm(ps(1, 0, 64), [(b2, csf), (("tlf", 0, 128), free)])
        NF = mm(ps(6, 100, 101), [(b2, sub(csf, 63, 64))])
        pre = tt(pv[3], ts(pv[2], q, 1024.0, AL.is_lt), free, AL.subtract)
        tq1 = tt(tile("tq1"), pre, a1, AL.mult)
        tq = add(tile("tq"), tq1, -1)
        tql = add(tile("tql"), tt(tile("tql0"), tq1, tt(pv[4], av, q, AL.is_lt), AL.mult), -1)
        mn = tt(tile("mn"), av, q, AL.min)
        nf = aff(tile("nf", 1), NF, 0.5, 0.0)
        hf = aff(pv[5], RF, 0.5, 6784.0, eng="V")
        s0 = tt(tile("s0"), hf, a78, AL.max)
        odd = ts(tile("odd", 64, "n"), ts(tile("ri", 64, "n"), hf, 1.0, AL.add), 1, AL.bitwise_and)
        ev = tt(tile("ev"), hf, odd, AL.subtract)
        g0 = tt(tile("g0"), aff(pv[3], ev, 1.0, 2049.0, eng="V"), free, AL.mult)
        pu = tt(tile("pu"), LQ, tql, AL.is_equal)
        far = ts(pv[6], D, sub(thr, rd, rd + 1), AL.is_ge)
        cand = tt(tile("cand", 64, "h"), pu, far, AL.mult)
        cs = scan(tile("cs", 64, "h"), ones, cand, AL.mult, AL.add)
        RC = mm(ps(2, 0, 64), [(b2, c212), (b2, cs), (("tlc", 0, 128), cand)])
        RI = mm(ps(1, 64, 128), [(b2, cs), (("tl", 0, 128), cand)])
        NC = mm(ps(6, 103, 104), [(b2, sub(cs, 63, 64))])
        cell = u16("cell" + R, tt(tile("cell"), RC, s0, AL.max), -7807)
        g1 = u16("g1" + R, tt(tile("g1"), RC, g0, AL.max), -8831)
        tab = ("big", TAB, IDP)
        scat(tab, cell, Lp, ("idc", 0, A))
        gat(("big", G1, TAB), tab, g1, name="G1", ch=512)
        room = ts(tile("room"), RI, nf, AL.is_le)
        zc = tile("zc", 1)
        op("red", "V", ("ew", 64, 64), [room], [zc],
           lambda g, T, qq, room=room, zc=zc: g.vector.tensor_reduce(ap(T, zc), ap(T, room), AxisListType.X, AL.add))
        cut = mm(ps(6, 102, 103), [(bf, zc)])
        pair = tt(tile("pair"), LQ, tq, AL.is_equal)
        cpr = tt(pv[7], pair, far, AL.mult)
        an = tt(slot(PM, 1, 4), pair, cpr, AL.subtract)
        aff(slot(PJ, 2, 3), an, -1.0, 1.0)
        aff(slot(PK, 3, 4), an, -1.0, 1.0)
        dbl = tt(slot(PJ, 1, 3), ts(tile("dbl0"), mn, cut, AL.is_lt), cpr, AL.mult)
        lim = ts(tile("lim", 1), NC, nf, AL.min)
        used = tt(slot(PU, 1, 2), ts(pv[2], ev, -8831.0, AL.add, lim, AL.is_le), free, AL.mult)
        W1 = ("big", LW, G1)
        add(slot(VJ1, 0, 3), qc, IPB - LW)
        add(slot(VJ1, 2, 3), locq, SEC)
        gat(("big", JA, JA + A), W1, u16("j1" + R, pick("j1", PJ, VJ1, 3)), name="J0a")
        tt(slot(VJ2, 0, 3), RC, add(tile("y0"), qc, G1 - LW), AL.max)
        add(slot(VJ2, 2, 3), locq, 2 * SEC)
        gat(("big", JA + A, IDB), ("big", LW, IDP), u16("j2" + R, pick("j2", PJ, VJ2, 3)), name="J0b", ch=512)
        dml = u16("dm" + R, tt(tile("dm"), an, a16, AL.mult))
        if rd == 0:
            gat(("sa", 16 + A, 16 + 2 * A), (xw, XZ, XL), dml, name="difm")
            for dst in (("sa", 16 + 2 * A, 16 + 3 * A), ("sc0", 0, A)):
                twin(dst, ("sa", 16 + A, 16 + 2 * A))
        else:
            gat(("difm", 0, A), (xw, XZ, XL), dml, name="difm")
            for i in (1, 2):
                t = tt(tile("sl%d" % i), aff(pv[4], qc, 1.0, float(H0 + i * A), eng="V"), an, AL.mult)
                gat(("sa", 16 + i * A, 16 + (i + 1) * A), ("ph1", 0, HZ), u16("su%d" % i, t), ("difm", 0, A), name="S")
        wins = (("big", IDP), ("jb", 0))
        sw = ("sa", "sb")
        KO = IDP - I1
        for lv in range(4):
            (b0, z0), (b1, z1) = wins[lv % 2], wins[1 - lv % 2]
            lst = tile("jl%d%d" % (rd, lv), 128, "u")
            for k in (0, 1):
                pw = wrap(ps(4 + k, 0, 64), (b0, z0 + (1 + k) * A, z0 + (2 + k) * A))
                cp(sub(lst, 64 * k, 64 * k + 64), pw)
                if lv == 0 and k == 1:
                    aff(slot(VK2, 1, 4), pw, 1.0, float(I1B - I1), eng="V")
            gat((b1, z1 + A, z1 + 3 * A), (b0, z0, z0 + P), lst, name="J%d" % lv)
            s0_, s1_ = sw[lv % 2], sw[1 - lv % 2]
            sc = "sc%d" % (lv % 2)
            if rd + lv > 0:
                twin((sc, 0, 2 * A), (s0_, 16 + A, 16 + 3 * A))
            for k in (0, 1):
                o = k * A if rd + lv > 0 else 0
                gat((s1_, 16 + (1 + k) * A, 16 + (2 + k) * A), (s0_, 16, 16 + P), sub(lst, 64 * k, 64 * k + 64),
                    (sc, o, o + A), name="S%d" % lv)
            if lv > 0:
                continue
            gv = wrap(ps(6, 0, 64), ("big", G1, TAB))
            gu = wrap(ps(1, 128, 192), ("big", G1, TAB), "e23")
            mf = tt(tile("mf"), gu, tt(tile("mf0"), gv, odd, AL.mult), AL.max)
            au = tt(slot(PM, 2, 4), an, used, AL.add)
            ov = tt(slot(PM, 3, 4), au, dbl, AL.add)
            keep = aff(slot(PK, 1, 4), ov, -1.0, 1.0)
            aff(slot(PK, 2, 4), au, -1.0, 1.0)
            tt(slot(VX, 0, 2), aff(tile("xe"), ev, 0.5, 1040.0 - 4416.5), ts(pv[4], odd, 256.0, AL.mult), AL.add)
            xl = u16("xl" + R, pick("xl", PU, VX, 2))
            f = 16.0 if rd == 0 else 1.0
            aff(slot(VM, 0, 4), a, f, f * (IPB - LW))
            add(slot(VM, 1, 4), mf, 2 * A)
            add(slot(VM, 2, 4), qc, A)
            src = pick("src", PM, VM, 4)
            gat(("mp", 0, A), W1, u16("mp" + R, turn("srcp", src) if rd == 0 else src), name="Mp")
            add(("big", T2, I1B), ("big", TAB + 1026, TAB + 1538), hc[2048])
            kl = tile("kl" + R, 200, "u")
            ml = tile("ml" + R, 200, "u")
            mo = 16 - 8 * rd
            pw = wrap(ps(7, 0, 64), ("mp", 0, A))
            for dst, s in ((0, pw), (192, sub(Lw, 192, 200))):
                ts(sub(kl, dst, dst + size(s)), s, float(KO), AL.add)
                ts(sub(ml, dst, dst + size(s)), s, float(mo), AL.add)
            add(slot(VK1, 0, 4), sub(Lw, 64, 128), KO)
            add(slot(VK1, 1, 4), qc, I1B - I1)
            add(slot(VK1, 2, 4), mf, A)
            add(slot(VK2, 0, 4), sub(Lw, 128, 192), KO)
            add(slot(VK2, 2, 4), tt(tile("tw"), ev, odd, AL.subtract), T2 - I1 - 8832)
            cp(sub(kl, 64, 128), pick("k1", PK, VK1, 4))
            cp(sub(kl, 128, 192), pick("k2", PK, VK2, 4))
            l16 = add(tile("l16", 128), sub(Lw, 64, 192), mo)
            mq = tile("mq", 128)
            for i in (0, 64):
                tt(sub(mq, i, i + 64), sub(l16, i, i + 64), keep, AL.mult)
            cp(sub(ml, 64, 192), mq)
            if rd == 1:
                gat(("hsrc", 0, A), ("ph1", H0, HD), u16("hl", src, 3 * A, AL.min), name="hsrc")
            wrap(ps(0, 64, 80), ("big", TAB + 2051, TAB + 2563), "e01", 2)
            wrap(ps(0, 80, 96), ("big", TAB + 2051, TAB + 2563), "e23", 2)
            vu = u16("vu" + R, ps(0, 64, 96))
            xu, xs, xf = tile("xu", 256, "h"), tile("xs", 256, "h"), tile("xf", 256, "h")
            gat(xu, x, sub(vu, 16, 32), name="xu")
            gat(xs, x, sub(vu, 0, 16), xu, name="xs")
            ts(xf, xs, 16.0, AL.is_ge, -16.0, AL.mult)
            scan((xw, XS, XS + 256), xf, xs, AL.min, AL.add)
            gat((xw, XS + 256, XZ), (xw, XD, XL), sub(vu, 16, 32), name="xd")
            gat((xn, X0, X0 + A), (xw, X0, XZ), xl, name="xn")
        KW = ("big", I1, BIGN)
        kbd = ("lr", 2 * A, 2 * A + NB)
        gat(kbd, KW, sub(kl, 192, 200), name="Kb")
        gat(("lp", 0, A), KW, sub(kl, 0, 64), name="Kp", ch=512)
        gat(("lr", 0, 2 * A), KW, sub(kl, 64, 192), name="Ka")
        rl = tile("rl" + R, 200, "u")
        pc = wrap(ps(6, 0, 8), kbd)
        cl = u16("cl" + R, pc, 1024, AL.min)
        ts(sub(rl, 192, 200), pc, 256.0, AL.add)
        aff(sub(V24, 0, 8), pc, 1.0, 256.0, eng="V")
        add(sub(V24, 8, 16), sub(V24, 0, 8), A)
        lc = tile("lc", 128, "h")
        gat(lc, ("lp", 0, A + 16), cl, name="lc")
        snd, rcv = "snd" + R, "rcv" + R
        gat((snd, 0, 128), (xn, X0, XS), cl, name="xc")
        pl = wrap(ps(2, 304, 312), lc)
        for i in (128, 136, 144):
            tt((snd, i, i + 8), pl, kw, AL.is_equal)
        remote(2 * rd, rd, (snd, 0, 152), (rcv, 0, 152))
        vf = tt(tile("vf", 24), V24, (snd, 128, 152), AL.mult)
        ts(sub(rl, 0, 64), wrap(ps(4, 0, 64), ("lp", 0, A)), 256.0, AL.add)
        ts(sub(rl, 64, 128), wrap(ps(5, 0, 64), ("lr", 0, A)), 256.0, AL.add)
        ts(sub(rl, 128, 192), wrap(ps(7, 0, 64), ("lr", A, 2 * A)), 256.0, AL.add)
        pb = "ph1" if rd == 0 else "ypb"
        phb = (pb, HB, HN)
        for (s, e, h) in ((3 * A, P, HB), (0, A, H0), (A, 2 * A, H0 + A), (2 * A, 3 * A, H0 + 2 * A)):
            lst = sub(ml, s // 16, e // 16)
            if rd == 0:
                gat((pb, h, h + e - s), ("sa", 0, 16 + P), lst, name="Q")
                continue
            base = ("hsrc", 0, A) if s == 0 else ("ph1", h, h + e - s)
            gat(("qi", s, e), ("sa", 8, 16 + P), lst, base, name="Q")
            ts(("qi", s, e), ("qi", s, e), -65521, AL.bitwise_and)
            ts((pb, h, h + e - s), ("qi", s, e), 0.0, AL.max)
        if rd == 0:
            aff(("cd0", 128, 256), kbd, m01, 0.0)
            add(("cd0", 0, 128), ("cd0", 128, 256), h01)
        else:
            add(("cd1", 128, 256), mm(ps(2, 128, 256), [(("b01", 0, 128), kbd)]), 0)
            add(("cd1", 0, 128), ("cd1", 128, 256), A)
        rcp = ("rcp" + R, 0, 128)
        remote(2 * rd + 1, rd, phb, rcp)
        cu = u16("cu" + R, tt(tile("c24", 24), tt(tile("c23", 24), vf, (rcv, 128, 152), AL.mult), K24, AL.max))
        c1, c2, c12, c3 = sub(cu, 0, 8), sub(cu, 8, 16), sub(cu, 0, 16), sub(cu, 16, 24)
        rho = "rho" + R
        scat((rho, 0, 256 + 2 * A), c12, ("cd" + R, 0, 256))
        lb = "big" if rd == 0 else "ylb"
        for (s, e) in ((A, 2 * A), (0, A), (2 * A, 3 * A), (3 * A, P)):
            gat((lb, 256 + s, 256 + e), (rho, 0, 3456), sub(rl, s // 16, e // 16), name="rm")
        lsw = (lb, 0, 256 + 2 * A)
        gat(("sw" + R, 0, 128), lsw, c2, name="swg")
        scat(lsw, c12, ("sw" + R, 0, 256))
        scat((xn, 0, X0 + A), c1, (rcv, 0, 128))
        sp = "sp" + R
        psw = (pb, 16, H0 + 2 * A)
        gat((sp, 0, 128), psw, c2, name="spg")
        si = tt(tile("si", 128, "n"), phb, rcp, AL.add)
        cp((sp, 128, 256), ts(si, si, 15, AL.bitwise_and))
        scat(psw, c12, (sp, 0, 256))
        scat((pb, HD, HN), c3, (sp, 128, 256))
        if rd == 0:
            Lw = tile("Lw1", 200)
            aff(sub(Lw, 0, 64), wrap(ps(0, 0, 64), ("big", LW, LW + A)), 1.0, 0.0, eng="V")
            add(sub(Lw, 64, 200), wrap(ps(6, 0, 136), ("big", LW + A, I1)), 0)
    for s, e, h in ((2 * A, 3 * A, H0 + 2 * A), (0, A, H0), (A, 2 * A, H0 + A), (3 * A, P, HB)):
        dma("Y", lambda T, s=s, e=e: T.yp[:, s:e], lambda T, h=h, n=e - s: T.ypb[:, h:h + n],
            [("ypb", h, h + e - s)], [], 256 * (e - s))
    for s, e in ((2 * A, P), (0, 2 * A)):
        dma("Y", lambda T, s=s, e=e: T.yl[:, s:e], lambda T, s=s, e=e: T.ylb[0:128:16, 256 + s:256 + e],
            [("ylb", 256 + s, 256 + e)], [], 32 * (e - s))
    dma("Y", lambda T: T.yx[:, :], lambda T: T.xw2[:, X0:X0 + A], [("xw2", X0, X0 + A)], [], 262144)
    assert top["w"] <= NW and top["u"] <= NU and top["n"] <= NI and top["h"] <= NH, top
    return ops


def depend(ops):
    deps = []
    seen = {}
    for j, o in enumerate(ops):
        d = set()
        acc = [(r, False) for r in o["rd"]] + [(r, True) for r in o["wr"]]
        for r, w in acc:
            bank = inps(r)
            for (i, r2, w2) in seen.get(r[0], ()):
                meet = (w or w2) and r[1] < r2[2] and r2[1] < r[2]
                if bank:
                    if meet or ops[i]["eng"] != o["eng"] or len(o["eng"]) > 1:
                        d.add(i)
                elif meet and not (len(r) > 4 and len(r2) > 4 and r[4] != r2[4]):
                    d.add(i)
        for r, w in acc:
            seen.setdefault(r[0], []).append((j, r, w))
        if o["name"] == "recv":
            d = {o["cost"][2]}
        d.discard(j)
        deps.append(sorted(d))
    return deps


def cost(o, q, m):
    c = o["cost"]
    ov = m["ov"] if q == "V" else m["oa"]
    if c[0] == "twin":
        if q == "Y":
            return 60.0, m["dma"] + c[1] * c[2] * 512 / m["bw"]
        t = ov + c[1] * (c[2] if q == "V" else 1.0) * m["cy"]
    elif c[0] == "ew":
        t = ov + (c[1] if q == "V" else c[2]) * m["cy"]
    elif c[0] == "gat":
        t = ov + c[1] * m["c"] * m["cy"]
    elif c[0] == "scat":
        t = ov + c[1] * m["s"] * m["cy"]
    elif c[0] == "pe":
        t = 50.0 + c[1] * m["pe"]
    elif c[0] == "g":
        t = c[1] + c[2] * m["cy"]
    elif c[0] == "dma":
        return 60.0, m["dma"] + c[1] / m["bw"]
    elif c[0] == "send":
        return 600.0, m["rem"] * 0.7
    else:
        return 0.0, m["rem"] * 0.3
    return t, t


def place(n, deps, succ, key, eng, du, tot, lat):
    left = [len(d) for d in deps]
    bs = {q: [] for q in "VSPGYR"}
    st = [0.0] * n
    fin = [0.0] * n
    rank = sorted(range(n), key=lambda j: key[j])
    at = [0] * n
    for p, j in enumerate(rank):
        at[j] = p
    for p in range(n):
        todo = [rank[p]]
        while todo:
            j = todo.pop()
            if left[j] != 0:
                continue
            left[j] = -1
            t = 0.0
            for i in deps[j]:
                if fin[i] > t:
                    t = fin[i]
            t += lat
            q = eng[j]
            d = du[j][q]
            b = bs[q]
            k = len(b)
            while k > 0 and b[k - 1][1] > t:
                k -= 1
            while k < len(b) and t + d > b[k][0]:
                if b[k][1] > t:
                    t = b[k][1]
                k += 1
            b.insert(k, (t, t + d, j))
            st[j] = t
            fin[j] = t + tot[j][q]
            for s in succ[j]:
                left[s] -= 1
                if left[s] == 0 and at[s] < p:
                    todo.append(s)
    return bs, st, fin


def plan(ops, deps, m, cfg):
    n = len(ops)
    anc = []
    for j in range(n):
        s = set(deps[j])
        for i in deps[j]:
            s |= anc[i]
        anc.append(s)
    deps = [[i for i in d if not any(i in anc[k] for k in d)] for d in deps]
    succ = [[] for _ in ops]
    for j in range(n):
        for i in deps[j]:
            succ[i].append(j)
    du = [{q: cost(o, q, m)[0] for q in o["eng"]} for o in ops]
    tot = [{q: cost(o, q, m)[1] for q in o["eng"]} for o in ops]
    lat = m["lat"]
    eng = [o["eng"][0] for o in ops]
    key = [0.0] * n
    for j in range(n - 1, -1, -1):
        key[j] = min([key[k] for k in succ[j]] + [0.0]) - tot[j][eng[j]] - lat
    rng = np.random.default_rng(cfg["seed"])
    flex = [j for j in range(n) if len(ops[j]["eng"]) > 1]
    big = [j for j in flex if ops[j]["cost"][0] != "ew"]
    bs, st, fin = place(n, deps, succ, key, eng, du, tot, lat)
    cur = max(fin)
    best = (cur, bs, eng)
    its = cfg["its"]
    for it, r in enumerate(rng.random((its, 6)).tolist()):
        k2, e2 = key, eng
        if r[0] < 0.3:
            pool = big if r[1] < 0.6 else flex
            j = pool[int(r[2] * len(pool))]
            e2 = list(eng)
            e2[j] = ops[j]["eng"].replace(eng[j], "")[int(r[3] * (len(ops[j]["eng"]) - 1))]
        elif r[0] < 0.36:
            f2 = place(n, succ, deps, [-f for f in fin], eng, du, tot, lat)[2]
            k2 = [-f for f in f2]
        else:
            a = int(r[1] * n)
            sh = (r[2] - 0.5) * (2000.0, 8000.0, 30000.0)[int(r[3] * 3)]
            k2 = list(key)
            for j in range(a, min(n, a + 1 + int(r[4] * r[4] * 14))):
                k2[j] += sh
        bs, st, f2 = place(n, deps, succ, k2, e2, du, tot, lat)
        t = max(f2)
        if t <= cur + cfg["heat"] * r[5] * (1.0 - it / its):
            cur, eng, fin = t, e2, f2
            key = st if r[4] < 0.3 else k2
            if t < best[0]:
                best = (t, bs, e2)
    return {q: [b[2] for b in best[1][q]] for q in best[1]}, best[2], best[0]


CACHE = {}


def rank_program(g, core, T, topo):
    rank = T.rank_of(core)
    if rank is None:
        return
    if "p" not in CACHE:
        ops = build(CFG)
        deps = depend(ops)
        CACHE["p"] = (ops, deps) + plan(ops, deps, NOM, CFG)
    ops, deps, order, where, _ = CACHE["p"]
    peers = [T.cores[rank ^ m] for m in XM]
    eng = [e for e in topo.engines(core, peers[0]) if e in topo.engines(core, peers[1])]
    mask = sum(1 << e for e in eng)
    mark = {}
    nd = 0
    for q in "VSPGY":
        c = 0
        for j in order[q]:
            if q == "Y" or ops[j]["name"] in ("dma", "send"):
                mark[j] = ("d%d" % nd, len(eng) if ops[j]["name"] == "send" else 16)
                nd += 1
            else:
                c += 1
                mark[j] = ("e" + q, c)
    for j in order["R"]:
        mark[j] = ("r%d" % ops[j]["cost"][1], len(eng))
    queue = {"V": g.vector, "S": g.scalar, "P": g.tensor, "G": g, "Y": g.sync}
    for q in "YSVPG":
        got = {}
        for j in order[q]:
            need = {}
            for i in deps[j]:
                s, c = mark[i]
                if c > got.get(s, 0) and c > need.get(s, 0):
                    need[s] = c
            for s, c in need.items():
                queue[q].wait_ge(T.sem[s], c)
                got[s] = c
            o = ops[j]
            if o["name"] == "send":
                src, dst = o["emit"]
                rid, pid, _ = topo.addr(peers[o["cost"][2]])
                g.remote_dma(ap(T, dst), ap(T, src), T.sem["r%d" % o["cost"][1]], T.sem[mark[j][0]], pid, rid, mask)
            else:
                o["emit"](g, T, q).then_inc(T.sem[mark[j][0]], 16 if mark[j][0][0] == "d" else 1)
        if q == "G":
            last = {}
            for s, c in mark.values():
                last[s] = max(last.get(s, 0), c)
            for s, c in last.items():
                if c > got.get(s, 0):
                    g.wait_ge(T.sem[s], c)
